import numpy as np
import ml_dtypes


def mxq(x, axis, fmt="e4m3"):
    dtype, down = {"e4m3": (ml_dtypes.float8_e4m3fn, 7), "e5m2": (ml_dtypes.float8_e5m2, 14)}[fmt]
    v = np.moveaxis(np.asarray(x, np.float32).astype(ml_dtypes.bfloat16).astype(np.float64), axis, -1)
    blocks = v.reshape(v.shape[:-1] + (-1, 32))
    amax = np.abs(blocks).max(-1, keepdims=True)
    byte = np.maximum(np.where(amax > 0, np.frexp(amax)[1] - 1 + 127, 0) - down, 1)
    scale = np.exp2(byte - 127.0)
    codes = (blocks / scale).astype(np.float32).astype(dtype).astype(np.float64)
    return np.moveaxis((codes * scale).reshape(v.shape), -1, axis)


WIDE = False


def mx_kscale(k):
    if not WIDE:
        return np.ones(k)
    levels = np.array([10, -10, 5, -5, 0])
    if k % 512:
        return np.exp2(np.random.permutation(np.resize(levels, k // 32))).repeat(32)
    a = np.empty((k // 512, 16))
    for p in range(k // 512):
        a[p, :8] = np.random.permutation(np.resize(levels, 8))
        for g in range(8):
            far = levels[np.abs(levels - a[p, g]) >= 10]
            a[p, g + 8] = far[np.random.randint(len(far))]
    return np.exp2(a.ravel()).repeat(32)


def f64(x):
    return np.asarray(x).astype(np.float64)


def striped(idx):
    return np.tile(idx.reshape(-1, 16).T, (8, 1)).astype(np.uint16)


def unstriped(offs):
    return offs[:16].T.reshape(-1).astype(np.int64)


def striped8(idx):
    return np.concatenate([x.reshape(-1, 16).T for x in idx]).astype(np.uint16)


def runs(offs, k):
    lists = np.stack([offs[16 * r : 16 * r + 16].T.reshape(-1) for r in range(8)]).astype(np.int64)
    return lists[np.arange(k) % 512 // 64]


def pack_weight(w):
    k, n = w.shape
    w = f64(np.asarray(w, np.float32).astype(ml_dtypes.bfloat16)).reshape(k // 32, 32, n)
    amax = np.abs(w).max(1)
    byte = np.clip(np.where(amax > 0, np.frexp(amax)[1] - 1 + 127 - 7, 1), 1, 254)
    scaled = (w * np.exp2(127.0 - byte)[:, None, :]).reshape(k, n).astype(np.float32)
    words = np.ascontiguousarray(scaled.reshape(k // 512, 128, 4, n).transpose(0, 1, 3, 2)).astype(ml_dtypes.float8_e4m3fn).view(np.uint8)
    return words, np.ascontiguousarray(byte.astype(np.uint8).reshape(k // 512, 16, n))


def unpack_weight(words, scales):
    g, p, n, _ = words.shape
    vals = np.ascontiguousarray(words).view(ml_dtypes.float8_e4m3fn).astype(np.float64) * np.repeat(np.exp2(scales.astype(np.float64) - 127.0), 8, axis=1)[..., None]
    return vals.transpose(0, 1, 3, 2).reshape(g * 512, n)


def sigmoid(v):
    return 1.0 / (1.0 + np.exp(-np.maximum(v, -700.0)))


K, T, S, H, W, G = 512, 2048, 512, 512, 256, 2048


def setup_inputs():
    n = np.random.standard_normal
    s = mx_kscale(K)[:, None]
    packed_xT = pack_weight(n((K, T)) * s)
    packed_dT = pack_weight(n((K, G)) / s)
    perm = np.stack([np.random.permutation(S) for _ in range(8)])
    return {
        "x_words": packed_xT[0],
        "x_scales": packed_xT[1],
        "w1": (n((K, H)) / np.sqrt(K) / s).astype(np.float32),
        "gs": (np.random.uniform(0.5, 1.5, (K, 1)) * s).astype(np.float32),
        "d_words": packed_dT[0],
        "d_scales": packed_dT[1],
        "offs": striped(np.random.permutation(T)[:S]),
        "n1": striped8(perm[:, :W]),
        "n2": striped8(perm[:, W:]),
        "k1": striped8(np.random.randint(0, G, (8, H))),
        "n3": striped8(np.stack([np.random.permutation(S) for _ in range(8)])),
        "n4": striped8(np.stack([np.random.permutation(S) for _ in range(8)])),
    }


def reference(x_words, x_scales, w1, gs, d_words, d_scales, offs, n1, n2, k1, n3, n4):
    d_k1 = unpack_weight(d_words, d_scales)[np.arange(K)[:, None], runs(k1, K)]
    xq = unpack_weight(x_words, x_scales)[:, unstriped(offs)]
    y = mxq(f64(w1), 0, "e4m3").T @ xq
    pa = y[np.arange(H)[:, None], runs(n1, H)]
    pb = y[np.arange(H)[:, None], runs(n2, H)]
    rb = pa - pb
    ra = 0.75 * (pa + pb)
    ds = np.zeros((H, S))
    ds[np.arange(H)[:, None], runs(n1, H)] = ra
    dt = ds.copy()
    dt[np.arange(H)[:, None], runs(n2, H)] = rb
    z = f64(gs) * dt
    h = 0.0625 * ((d_k1.T @ mxq(z, 0, "e4m3")))
    return (h - (h[np.arange(H)[:, None], runs(n3, H)])) * (sigmoid(h[np.arange(H)[:, None], runs(n4, H)]))

@@ -1,0 +1,252 @@
+from contextlib import ExitStack
+
+import concourse.mybir as mybir
+
+K, T, S, H, W, G = 512, 2048, 512, 512, 256, 2048
+FLOPS = 2 * K * H * S + 2 * K * H * S
+
+F32 = mybir.dt.float32
+BF16 = mybir.dt.bfloat16
+I32 = mybir.dt.int32
+U32 = mybir.dt.uint32
+U16 = mybir.dt.uint16
+U8 = mybir.dt.uint8
+FP8X4 = mybir.dt.float8_e4m3fn_x4
+ADD = mybir.AluOpType.add
+SUB = mybir.AluOpType.subtract
+MULT = mybir.AluOpType.mult
+COPY = mybir.ActivationFunctionType.Copy
+SIGMOID = mybir.ActivationFunctionType.Sigmoid
+
+P = 128
+PACK = 4
+HALF = S // 2
+M = 128
+
+
+def tile_picked_densehaargdif_none_p_kernel(
+    tc, x_words, x_scales, w1, gs, d_words, d_scales, offs, n1, n2, k1, n3, n4, out
+):
+    nc = tc.nc
+    with ExitStack() as ctx:
+        lists = ctx.enter_context(tc.tile_pool(name="lists", bufs=1))
+        keep = ctx.enter_context(tc.tile_pool(name="keep", bufs=1))
+        psum = ctx.enter_context(tc.psum_pool(name="psum", bufs=1))
+
+        def sb(name, shape, dtype, tag=None):
+            return keep.tile(shape, dtype, name=name, tag=tag or name, align_bytes=64)
+
+        offs_t = lists.tile([P, S // 16], U16, name="offs_t")
+        n1_t = lists.tile([P, W // 16], U16, name="n1_t")
+        n2_t = lists.tile([P, W // 16], U16, name="n2_t")
+        k1_t = lists.tile([P, H // 16], U16, name="k1_t")
+        n3_t = lists.tile([P, S // 16], U16, name="n3_t")
+        n4_t = lists.tile([P, S // 16], U16, name="n4_t")
+
+        w_raw = sb("w_raw", [P, PACK, H], F32)
+        xw = sb("xw", [P, T], U32)
+        xs = sb("xs", [P, T], U8)
+        dw = sb("dw", [P, G], U32)
+        ds = sb("ds", [P, G], U8)
+        gain = sb("gain", [P, PACK], F32)
+        d_scale = sb("d_scale", [P, H], U8)
+
+        nc.gpsimd.memset(xs[:].bitcast(I32), 0)
+        nc.vector.memset(ds[:].bitcast(I32), 0)
+        nc.vector.memset(d_scale[:].bitcast(I32), 0)
+
+        nc.sync.dma_start(w_raw[:], w1.rearrange("(p j) c -> p j c", j=PACK))
+        nc.sync.dma_start(offs_t[:], offs)
+        for q in range(4):
+            nc.sync.dma_start(
+                xs[32 * q : 32 * q + 4, :].bitcast(I32), x_scales[0, 4 * q : 4 * q + 4, :].bitcast(I32)
+            )
+        nc.sync.dma_start(xw[:].bitcast(I32), x_words[0].rearrange("p n t -> p (n t)").bitcast(I32))
+        nc.sync.dma_start(k1_t[:], k1)
+        nc.gpsimd.dma_start(gain[:], gs.rearrange("(p t) o -> p (t o)", t=PACK))
+        d_rows = d_scales[0].rearrange("(r s) c -> s r c", s=2)
+        for s in range(2):
+            nc.gpsimd.dma_start(ds[s:P:16, :].bitcast(I32), d_rows[s].bitcast(I32))
+        nc.sync.dma_start(n1_t[:], n1)
+        nc.sync.dma_start(n2_t[:], n2)
+        nc.sync.dma_start(dw[:].bitcast(I32), d_words[0].rearrange("p n t -> p (n t)").bitcast(I32))
+        nc.sync.dma_start(n3_t[:], n3)
+        nc.sync.dma_start(n4_t[:], n4)
+
+        x_scale = sb("x_scale", [P, S], U8)
+        nc.vector.tensor_copy(x_scale[:], xs[:].indirect(offs_t[:]))
+
+        w_view = w_raw[:].rearrange("p j (m a e) -> p e m j a", a=2, e=2)
+        w_codes, w_scales, w_bf = {}, {}, {}
+        for e in (1, 0):
+            w_bf[e] = sb(f"w_bf{e}", [P, 2 * M * PACK], BF16)
+            w_codes[e] = sb(f"w_codes{e}", [P, 2 * M], U32)
+            w_scales[e] = sb(f"w_scales{e}", [P, 2 * M], U8)
+        nc.vector.tensor_copy(w_bf[1][:].rearrange("p (a m j) -> p m j a", a=2, j=PACK), w_view[:, 1])
+        nc.scalar.copy(w_bf[0][:].rearrange("p (a m j) -> p m j a", a=2, j=PACK), w_view[:, 0])
+        for e in (1, 0):
+            nc.vector.quantize_mx(out=w_codes[e][:].bitcast(FP8X4), scales=w_scales[e][:], in_=w_bf[e][:])
+
+        x_codes = sb("x_codes", [P, S], U32)
+        for h in range(2):
+            nc.vector.tensor_copy(
+                x_codes[:, h * HALF : (h + 1) * HALF], xw[:].indirect(offs_t[:, h * 16 : (h + 1) * 16])
+            )
+
+        banks = [psum.tile([P, S], F32, name=f"bank{b}") for b in range(8)]
+
+        def product(bank_cols, lhs_codes, lhs_scales, rhs_codes, rhs_scales):
+            nc.tensor.matmul_mx(
+                out=bank_cols,
+                lhsT=lhs_codes.bitcast(FP8X4),
+                lhsT_scale=lhs_scales,
+                rhs=rhs_codes.bitcast(FP8X4),
+                rhs_scale=rhs_scales,
+                start=True,
+                stop=True,
+            )
+
+        order = (1, 3, 0, 2)
+        y = {}
+        for i, t in enumerate(order):
+            e, a = t % 2, t // 2
+            cols = slice(a * M, (a + 1) * M)
+            y[t] = sb(f"y{t}", [P, S], F32)
+            if i == 0:
+                for h in range(2):
+                    c = slice(h * HALF, (h + 1) * HALF)
+                    product(banks[h][:, :HALF], w_codes[e][:, cols], w_scales[e][:, cols], x_codes[:, c], x_scale[:, c])
+                    nc.scalar.activation(y[t][:, c], banks[h][:, :HALF], COPY, scale=gain[:, t : t + 1])
+            else:
+                product(banks[i + 1][:], w_codes[e][:, cols], w_scales[e][:, cols], x_codes[:], x_scale[:])
+
+        ds_picked = sb("ds_picked", [P, H], U8)
+        ds_dealt = sb("ds_dealt", [P, H], U8)
+        nc.vector.tensor_copy(ds_picked[:], ds[:].indirect(k1_t[:]))
+
+        dt = {
+            1: sb("dt1", [P, S], F32),
+            3: sb("dt3", [P, S], F32),
+            0: sb("dt01", [P, 2 * S], F32),
+            2: sb("dt23", [P, 2 * S], F32),
+        }
+        plain, scaled, wide = {}, {}, {}
+
+        def fetch(i, t):
+            plain[t] = sb(f"plain{t}", [P, 2, W], F32)
+            wide[t] = sb(f"wide{t}", [P, 2 * S], F32)
+            scaled[t] = wide[t][:, S:].rearrange("p (a w) -> p a w", a=2)
+            if i > 0:
+                nc.scalar.activation(y[t][:], banks[i + 1][:], COPY, scale=gain[:, t : t + 1])
+                nc.scalar.activation(plain[t][:, 0, :], y[t][:].indirect(n1_t[:]), COPY)
+            else:
+                nc.vector.tensor_copy(plain[t][:, 0, :], y[t][:].indirect(n1_t[:]))
+            nc.scalar.activation(plain[t][:, 1, :], y[t][:].indirect(n2_t[:]), COPY, scale=-1.0)
+
+        def scale(t):
+            nc.scalar.activation(scaled[t][:, 0, :], plain[t][:, 0, :], COPY, scale=0.75)
+            nc.scalar.activation(scaled[t][:, 1, :], plain[t][:, 1, :], COPY, scale=-0.75)
+
+        def put_difference(t):
+            nc.vector.tensor_tensor(dt[t][:].indirect(n2_t[:]), plain[t][:, 0, :], plain[t][:, 1, :], ADD)
+
+        def put_sum(t):
+            nc.vector.tensor_tensor(dt[t][:].indirect(n1_t[:]), scaled[t][:, 0, :], scaled[t][:, 1, :], ADD)
+
+        fetch(0, 1)
+        nc.vector.tensor_copy(
+            ds_dealt[:].rearrange("p (t m) -> p m t", t=PACK), ds_picked[:].rearrange("p (m t) -> p m t", t=PACK)
+        )
+        for o in range(2):
+            for s in range(2):
+                nc.sync.dma_start(
+                    d_scale[2 * o + s : P : 32, :].bitcast(I32), ds_dealt[16 * o + s : P : 32, :].bitcast(I32)
+                )
+        put_difference(1)
+        scale(1)
+        fetch(1, 3)
+        d_picked = sb("d_picked", [P, H], U32)
+        d_codes = sb("d_codes", [P, H], U32, tag="y3")
+        nc.vector.tensor_copy(d_picked[:], dw[:].indirect(k1_t[:]))
+        put_sum(1)
+        put_difference(3)
+        nc.vector.tensor_copy(
+            d_codes[:].rearrange("p (t m) -> p m t", t=PACK), d_picked[:].rearrange("p (m t) -> p m t", t=PACK)
+        )
+        scale(3)
+        fetch(2, 0)
+        nc.scalar.copy(dt[0][:, S:], dt[1][:])
+        put_sum(3)
+        put_difference(0)
+        fetch(3, 2)
+        nc.scalar.copy(dt[2][:, S:], dt[3][:])
+        scale(0)
+        put_difference(2)
+        scale(2)
+        put_sum(0)
+        put_sum(2)
+
+        z_bf = [sb(f"z_bf{h}", [P, HALF, PACK], BF16) for h in range(2)]
+        pair = {t: dt[t][:].rearrange("p (e n) -> p n e", e=2) for t in (0, 2)}
+        for h in range(2):
+            nc.scalar.copy(z_bf[h][:, :, 0:2], pair[0][:, h * HALF : (h + 1) * HALF, :])
+        nc.vector.tensor_copy(z_bf[0][:, :, 2:4], pair[2][:, :HALF, :])
+        nc.scalar.copy(z_bf[1][:, :, 2:4], pair[2][:, HALF:, :])
+        z_codes = sb("z_codes", [P, S], U32)
+        z_scales = sb("z_scales", [P, S], U8)
+        for h in range(2):
+            c = slice(h * HALF, (h + 1) * HALF)
+            nc.vector.quantize_mx(
+                out=z_codes[:, c].bitcast(FP8X4),
+                scales=z_scales[:, c],
+                in_=z_bf[h][:].rearrange("p n t -> p (n t)"),
+            )
+
+        out_rows = out.rearrange("(p t) n -> p t n", t=PACK)
+        sums = {}
+        for t in range(PACK):
+            cols = slice(t * M, (t + 1) * M)
+            if t == 0:
+                sums[t] = [banks[5][:, :HALF], banks[6][:, :HALF]]
+                for h in range(2):
+                    c = slice(h * HALF, (h + 1) * HALF)
+                    product(sums[t][h], d_codes[:, cols], d_scale[:, cols], z_codes[:, c], z_scales[:, c])
+            else:
+                bank = banks[(7, 0, 1)[t - 1]]
+                sums[t] = [bank[:, :HALF], bank[:, HALF:]]
+                product(bank[:], d_codes[:, cols], d_scale[:, cols], z_codes[:], z_scales[:])
+
+        for t in range(PACK):
+            hw = wide[t]
+            gate = sb(f"gate{t}", [P, S], F32)
+            other = sb(f"other{t}", [P, S], F32)
+            diff = sb(f"diff{t}", [P, S], F32)
+            res = sb(f"res{t}", [P, S], F32)
+            if t == 0:
+                nc.scalar.activation(hw[:, :HALF], sums[t][0], COPY, scale=0.0625)
+                nc.vector.tensor_scalar(hw[:, HALF:S], sums[t][1], 0.0625, None, MULT)
+            else:
+                nc.scalar.activation(hw[:, :S], banks[(7, 0, 1)[t - 1]][:], COPY, scale=0.0625)
+            if t < PACK - 1:
+                nc.scalar.activation(gate[:], hw[:].indirect(n4_t[:]), SIGMOID)
+                nc.vector.tensor_copy(other[:], hw[:].indirect(n3_t[:]))
+                if t == 0:
+                    for h in range(2):
+                        c = slice(h * HALF, (h + 1) * HALF)
+                        nc.vector.scalar_tensor_tensor(diff[:, c], sums[t][h], 0.0625, other[:, c], MULT, SUB)
+                else:
+                    nc.vector.scalar_tensor_tensor(diff[:], banks[(7, 0, 1)[t - 1]][:], 0.0625, other[:], MULT, SUB)
+                nc.gpsimd.tensor_tensor(res[:], diff[:], gate[:], MULT)
+                nc.sync.dma_start(out_rows[:, t, :], res[:])
+            else:
+                for h in range(2):
+                    c = slice(h * HALF, (h + 1) * HALF)
+                    nc.scalar.activation(gate[:, c], hw[:].indirect(n4_t[:, h * 16 : (h + 1) * 16]), SIGMOID)
+                    nc.vector.tensor_copy(other[:, c], hw[:].indirect(n3_t[:, h * 16 : (h + 1) * 16]))
+                for h in range(2):
+                    c = slice(h * HALF, (h + 1) * HALF)
+                    nc.vector.scalar_tensor_tensor(diff[:, c], sums[t][h], 0.0625, other[:, c], MULT, SUB)
+                for h in range(2):
+                    c = slice(h * HALF, (h + 1) * HALF)
+                    nc.vector.tensor_tensor(res[:, c], diff[:, c], gate[:, c], MULT)
+                    nc.sync.dma_start(out_rows[:, t, c], res[:, c])

@@ -106,83 +106,79 @@ def tile_picked_densehaargdif_none_p_kernel(
                 stop=True,
             )
 
-        order = (1, 3, 0, 2)
-        y = {}
-        for i, t in enumerate(order):
+        y, first, second, wide, dt = {}, {}, {}, {}, {}
+
+        def project(t):
             e, a = t % 2, t // 2
             cols = slice(a * M, (a + 1) * M)
             y[t] = sb(f"y{t}", [P, S], F32)
-            if i == 0:
+            if t == 1:
                 for h in range(2):
                     c = slice(h * HALF, (h + 1) * HALF)
                     product(banks[h][:, :HALF], w_codes[e][:, cols], w_scales[e][:, cols], x_codes[:, c], x_scale[:, c])
                     nc.scalar.activation(y[t][:, c], banks[h][:, :HALF], COPY, scale=gain[:, t : t + 1])
             else:
-                product(banks[i + 1][:], w_codes[e][:, cols], w_scales[e][:, cols], x_codes[:], x_scale[:])
+                product(banks[1][:], w_codes[e][:, cols], w_scales[e][:, cols], x_codes[:], x_scale[:])
+                nc.scalar.activation(y[t][:], banks[1][:], COPY, scale=gain[:, t : t + 1])
 
+        def fetch(t):
+            first[t] = sb(f"first{t}", [P, W], F32)
+            second[t] = sb(f"second{t}", [P, W], F32)
+            nc.scalar.activation(first[t][:], y[t][:].indirect(n1_t[:]), COPY)
+            nc.scalar.activation(second[t][:], y[t][:].indirect(n2_t[:]), COPY, scale=-1.0)
+
+        def scale(t):
+            wide[t] = sb(f"wide{t}", [P, 2 * S], F32)
+            nc.scalar.activation(wide[t][:, S + W :], second[t][:], COPY, scale=-0.75)
+            nc.scalar.activation(wide[t][:, S : S + W], first[t][:], COPY, scale=0.75)
+
+        def put_difference(t):
+            nc.vector.tensor_tensor(dt[t][:].indirect(n2_t[:]), first[t][:], second[t][:], ADD)
+
+        def put_sum(t):
+            nc.vector.tensor_tensor(dt[t][:].indirect(n1_t[:]), wide[t][:, S : S + W], wide[t][:, S + W :], ADD)
+
+        project(1)
         ds_picked = sb("ds_picked", [P, H], U8)
         ds_dealt = sb("ds_dealt", [P, H], U8)
         nc.vector.tensor_copy(ds_picked[:], ds[:].indirect(k1_t[:]))
-
-        dt = {
-            1: sb("dt1", [P, S], F32),
-            3: sb("dt3", [P, S], F32),
-            0: sb("dt01", [P, 2 * S], F32),
-            2: sb("dt23", [P, 2 * S], F32),
-        }
-        plain, scaled, wide = {}, {}, {}
-
-        def fetch(i, t):
-            plain[t] = sb(f"plain{t}", [P, 2, W], F32)
-            wide[t] = sb(f"wide{t}", [P, 2 * S], F32)
-            scaled[t] = wide[t][:, S:].rearrange("p (a w) -> p a w", a=2)
-            if i > 0:
-                nc.scalar.activation(y[t][:], banks[i + 1][:], COPY, scale=gain[:, t : t + 1])
-                nc.scalar.activation(plain[t][:, 0, :], y[t][:].indirect(n1_t[:]), COPY)
-            else:
-                nc.vector.tensor_copy(plain[t][:, 0, :], y[t][:].indirect(n1_t[:]))
-            nc.scalar.activation(plain[t][:, 1, :], y[t][:].indirect(n2_t[:]), COPY, scale=-1.0)
-
-        def scale(t):
-            nc.scalar.activation(scaled[t][:, 0, :], plain[t][:, 0, :], COPY, scale=0.75)
-            nc.scalar.activation(scaled[t][:, 1, :], plain[t][:, 1, :], COPY, scale=-0.75)
-
-        def put_difference(t):
-            nc.vector.tensor_tensor(dt[t][:].indirect(n2_t[:]), plain[t][:, 0, :], plain[t][:, 1, :], ADD)
-
-        def put_sum(t):
-            nc.vector.tensor_tensor(dt[t][:].indirect(n1_t[:]), scaled[t][:, 0, :], scaled[t][:, 1, :], ADD)
-
-        fetch(0, 1)
         nc.vector.tensor_copy(
             ds_dealt[:].rearrange("p (t m) -> p m t", t=PACK), ds_picked[:].rearrange("p (m t) -> p m t", t=PACK)
         )
+        fetch(1)
+        dt[1] = sb("dt1", [P, S], F32, tag="ds")
+        dt[3] = sb("dt3", [P, S], F32)
+        put_difference(1)
         for o in range(2):
             for s in range(2):
                 nc.sync.dma_start(
                     d_scale[2 * o + s : P : 32, :].bitcast(I32), ds_dealt[16 * o + s : P : 32, :].bitcast(I32)
                 )
-        put_difference(1)
         scale(1)
-        fetch(1, 3)
+        put_sum(1)
+        project(3)
+        fetch(3)
         d_picked = sb("d_picked", [P, H], U32)
         d_codes = sb("d_codes", [P, H], U32, tag="y3")
-        nc.vector.tensor_copy(d_picked[:], dw[:].indirect(k1_t[:]))
-        put_sum(1)
         put_difference(3)
+        nc.vector.tensor_copy(d_picked[:], dw[:].indirect(k1_t[:]))
+        scale(3)
+        put_sum(3)
+        project(0)
+        fetch(0)
+        dt[0] = sb("dt01", [P, 2 * S], F32, tag="y0")
+        nc.scalar.copy(dt[0][:, S:], dt[1][:])
+        put_difference(0)
         nc.vector.tensor_copy(
             d_codes[:].rearrange("p (t m) -> p m t", t=PACK), d_picked[:].rearrange("p (m t) -> p m t", t=PACK)
         )
-        scale(3)
-        fetch(2, 0)
-        nc.scalar.copy(dt[0][:, S:], dt[1][:])
-        put_sum(3)
-        put_difference(0)
-        fetch(3, 2)
-        nc.scalar.copy(dt[2][:, S:], dt[3][:])
+        project(2)
+        fetch(2)
         scale(0)
-        put_difference(2)
         scale(2)
+        dt[2] = sb("dt23", [P, 2 * S], F32, tag="y2")
+        nc.scalar.copy(dt[2][:, S:], dt[3][:])
+        put_difference(2)
         put_sum(0)
         put_sum(2)
 
@@ -216,6 +212,7 @@ def tile_picked_densehaargdif_none_p_kernel(
                 sums[t] = [bank[:, :HALF], bank[:, HALF:]]
                 product(bank[:], d_codes[:, cols], d_scale[:, cols], z_codes[:], z_scales[:])
 
+        halves = [slice(h * HALF, (h + 1) * HALF) for h in range(2)]
         for t in range(PACK):
             hw = wide[t]
             gate = sb(f"gate{t}", [P, S], F32)
@@ -227,26 +224,25 @@ def tile_picked_densehaargdif_none_p_kernel(
                 nc.vector.tensor_scalar(hw[:, HALF:S], sums[t][1], 0.0625, None, MULT)
             else:
                 nc.scalar.activation(hw[:, :S], banks[(7, 0, 1)[t - 1]][:], COPY, scale=0.0625)
+            if t % 2 == 0:
+                nc.vector.tensor_copy(other[:], hw[:].indirect(n3_t[:]))
+            else:
+                nc.vector.tensor_copy(other[:, :HALF], hw[:].indirect(n3_t[:, :16]))
+                nc.scalar.activation(other[:, HALF:], hw[:].indirect(n3_t[:, 16:]), COPY)
             if t < PACK - 1:
                 nc.scalar.activation(gate[:], hw[:].indirect(n4_t[:]), SIGMOID)
-                nc.vector.tensor_copy(other[:], hw[:].indirect(n3_t[:]))
                 if t == 0:
-                    for h in range(2):
-                        c = slice(h * HALF, (h + 1) * HALF)
+                    for h, c in enumerate(halves):
                         nc.vector.scalar_tensor_tensor(diff[:, c], sums[t][h], 0.0625, other[:, c], MULT, SUB)
                 else:
                     nc.vector.scalar_tensor_tensor(diff[:], banks[(7, 0, 1)[t - 1]][:], 0.0625, other[:], MULT, SUB)
-                nc.gpsimd.tensor_tensor(res[:], diff[:], gate[:], MULT)
+                nc.vector.tensor_tensor(res[:], diff[:], gate[:], MULT)
                 nc.sync.dma_start(out_rows[:, t, :], res[:])
             else:
-                for h in range(2):
-                    c = slice(h * HALF, (h + 1) * HALF)
+                for h, c in enumerate(halves):
                     nc.scalar.activation(gate[:, c], hw[:].indirect(n4_t[:, h * 16 : (h + 1) * 16]), SIGMOID)
-                    nc.vector.tensor_copy(other[:, c], hw[:].indirect(n3_t[:, h * 16 : (h + 1) * 16]))
-                for h in range(2):
-                    c = slice(h * HALF, (h + 1) * HALF)
+                for h, c in enumerate(halves):
                     nc.vector.scalar_tensor_tensor(diff[:, c], sums[t][h], 0.0625, other[:, c], MULT, SUB)
-                for h in range(2):
-                    c = slice(h * HALF, (h + 1) * HALF)
+                for h, c in enumerate(halves):
                     nc.vector.tensor_tensor(res[:, c], diff[:, c], gate[:, c], MULT)
                     nc.sync.dma_start(out_rows[:, t, c], res[:, c])

@@ -55,18 +55,18 @@ def tile_picked_densehaargdif_none_p_kernel(
         nc.vector.memset(ds[:].bitcast(I32), 0)
         nc.vector.memset(d_scale[:].bitcast(I32), 0)
 
-        nc.sync.dma_start(w_raw[:], w1.rearrange("(p j) c -> p j c", j=PACK))
         nc.sync.dma_start(offs_t[:], offs)
+        nc.sync.dma_start(w_raw[:], w1.rearrange("(p j) c -> p j c", j=PACK))
         for q in range(4):
             nc.sync.dma_start(
                 xs[32 * q : 32 * q + 4, :].bitcast(I32), x_scales[0, 4 * q : 4 * q + 4, :].bitcast(I32)
             )
         nc.sync.dma_start(xw[:].bitcast(I32), x_words[0].rearrange("p n t -> p (n t)").bitcast(I32))
         nc.sync.dma_start(k1_t[:], k1)
-        nc.gpsimd.dma_start(gain[:], gs.rearrange("(p t) o -> p (t o)", t=PACK))
         d_rows = d_scales[0].rearrange("(r s) c -> s r c", s=2)
         for s in range(2):
-            nc.gpsimd.dma_start(ds[s:P:16, :].bitcast(I32), d_rows[s].bitcast(I32))
+            nc.sync.dma_start(ds[s:P:16, :].bitcast(I32), d_rows[s].bitcast(I32))
+        nc.sync.dma_start(gain[:], gs.rearrange("(p t) o -> p (t o)", t=PACK))
         nc.sync.dma_start(n1_t[:], n1)
         nc.sync.dma_start(n2_t[:], n2)
         nc.sync.dma_start(dw[:].bitcast(I32), d_words[0].rearrange("p n t -> p (n t)").bitcast(I32))
@@ -122,46 +122,48 @@ def tile_picked_densehaargdif_none_p_kernel(
                 nc.scalar.activation(y[t][:], banks[1][:], COPY, scale=gain[:, t : t + 1])
 
         def fetch(t):
-            first[t] = sb(f"first{t}", [P, W], F32)
-            second[t] = sb(f"second{t}", [P, W], F32)
-            nc.scalar.activation(first[t][:], y[t][:].indirect(n1_t[:]), COPY)
-            nc.scalar.activation(second[t][:], y[t][:].indirect(n2_t[:]), COPY, scale=-1.0)
+            wide[t] = sb(f"wide{t}", [P, 2 * S], F32)
+            first[t] = wide[t][:, S : S + W]
+            second[t] = wide[t][:, S + W :]
+            if t == 1:
+                nc.vector.tensor_copy(first[t], y[t][:].indirect(n1_t[:]))
+            else:
+                nc.scalar.activation(first[t], y[t][:].indirect(n1_t[:]), COPY)
+            nc.scalar.activation(second[t], y[t][:].indirect(n2_t[:]), COPY, scale=-1.0)
 
         def scale(t):
-            wide[t] = sb(f"wide{t}", [P, 2 * S], F32)
-            nc.scalar.activation(wide[t][:, S + W :], second[t][:], COPY, scale=-0.75)
-            nc.scalar.activation(wide[t][:, S : S + W], first[t][:], COPY, scale=0.75)
+            scaled[t] = sb(f"scaled{t}", [P, 2 * W], F32)
+            nc.scalar.activation(scaled[t][:, :W], first[t], COPY, scale=0.75)
+            nc.scalar.activation(scaled[t][:, W:], second[t], COPY, scale=-0.75)
 
         def put_difference(t):
-            nc.vector.tensor_tensor(dt[t][:].indirect(n2_t[:]), first[t][:], second[t][:], ADD)
+            nc.vector.tensor_tensor(dt[t][:].indirect(n2_t[:]), first[t], second[t], ADD)
 
         def put_sum(t):
-            nc.vector.tensor_tensor(dt[t][:].indirect(n1_t[:]), wide[t][:, S : S + W], wide[t][:, S + W :], ADD)
+            nc.vector.tensor_tensor(dt[t][:].indirect(n1_t[:]), scaled[t][:, :W], scaled[t][:, W:], ADD)
 
+        scaled = {}
         project(1)
         ds_picked = sb("ds_picked", [P, H], U8)
-        ds_dealt = sb("ds_dealt", [P, H], U8)
         nc.vector.tensor_copy(ds_picked[:], ds[:].indirect(k1_t[:]))
-        nc.vector.tensor_copy(
-            ds_dealt[:].rearrange("p (t m) -> p m t", t=PACK), ds_picked[:].rearrange("p (m t) -> p m t", t=PACK)
-        )
         fetch(1)
         dt[1] = sb("dt1", [P, S], F32, tag="ds")
         dt[3] = sb("dt3", [P, S], F32)
         put_difference(1)
+        ds_dealt = sb("ds_dealt", [P, H], U8, tag="y1")
+        nc.vector.tensor_copy(
+            ds_dealt[:].rearrange("p (t m) -> p m t", t=PACK), ds_picked[:].rearrange("p (m t) -> p m t", t=PACK)
+        )
         for o in range(2):
             for s in range(2):
                 nc.sync.dma_start(
                     d_scale[2 * o + s : P : 32, :].bitcast(I32), ds_dealt[16 * o + s : P : 32, :].bitcast(I32)
                 )
-        scale(1)
-        put_sum(1)
         project(3)
         fetch(3)
-        d_picked = sb("d_picked", [P, H], U32)
-        d_codes = sb("d_codes", [P, H], U32, tag="y3")
         put_difference(3)
-        nc.vector.tensor_copy(d_picked[:], dw[:].indirect(k1_t[:]))
+        scale(1)
+        put_sum(1)
         scale(3)
         put_sum(3)
         project(0)
@@ -169,25 +171,31 @@ def tile_picked_densehaargdif_none_p_kernel(
         dt[0] = sb("dt01", [P, 2 * S], F32, tag="y0")
         nc.scalar.copy(dt[0][:, S:], dt[1][:])
         put_difference(0)
-        nc.vector.tensor_copy(
-            d_codes[:].rearrange("p (t m) -> p m t", t=PACK), d_picked[:].rearrange("p (m t) -> p m t", t=PACK)
-        )
         project(2)
         fetch(2)
-        scale(0)
-        scale(2)
         dt[2] = sb("dt23", [P, 2 * S], F32, tag="y2")
         nc.scalar.copy(dt[2][:, S:], dt[3][:])
         put_difference(2)
+        scale(0)
         put_sum(0)
+        scale(2)
         put_sum(2)
 
-        z_bf = [sb(f"z_bf{h}", [P, HALF, PACK], BF16) for h in range(2)]
-        pair = {t: dt[t][:].rearrange("p (e n) -> p n e", e=2) for t in (0, 2)}
+        pairs = sb("pairs", [P, 2, S, 2], BF16)
+        nc.scalar.copy(pairs[:, 0], dt[0][:].rearrange("p (e n) -> p n e", e=2))
         for h in range(2):
-            nc.scalar.copy(z_bf[h][:, :, 0:2], pair[0][:, h * HALF : (h + 1) * HALF, :])
-        nc.vector.tensor_copy(z_bf[0][:, :, 2:4], pair[2][:, :HALF, :])
-        nc.scalar.copy(z_bf[1][:, :, 2:4], pair[2][:, HALF:, :])
+            c = slice(h * HALF, (h + 1) * HALF)
+            nc.scalar.copy(pairs[:, 1, c, :], dt[2][:].rearrange("p (e n) -> p n e", e=2)[:, c, :])
+        pair_words = pairs[:].rearrange("p a n e -> p (a n e)").bitcast(U32).rearrange("p (a n) -> p n a", a=2)
+        z_bf = [sb(f"z_bf{h}", [P, HALF * PACK], BF16) for h in range(2)]
+        for h in range(2):
+            nc.scalar.copy(
+                z_bf[h][:].bitcast(U32).rearrange("p (n a) -> p n a", a=2), pair_words[:, h * HALF : (h + 1) * HALF, :]
+            )
+
+        d_picked = sb("d_picked", [P, H], U32, tag="scaled2")
+        d_codes = sb("d_codes", [P, H], U32)
+        nc.vector.tensor_copy(d_picked[:], dw[:].indirect(k1_t[:]))
         z_codes = sb("z_codes", [P, S], U32)
         z_scales = sb("z_scales", [P, S], U8)
         for h in range(2):
@@ -195,54 +203,72 @@ def tile_picked_densehaargdif_none_p_kernel(
             nc.vector.quantize_mx(
                 out=z_codes[:, c].bitcast(FP8X4),
                 scales=z_scales[:, c],
-                in_=z_bf[h][:].rearrange("p n t -> p (n t)"),
+                in_=z_bf[h][:],
             )
+            if h == 0:
+                nc.vector.tensor_copy(
+                    d_codes[:].rearrange("p (t m) -> p m t", t=PACK),
+                    d_picked[:].rearrange("p (m t) -> p m t", t=PACK),
+                )
 
         out_rows = out.rearrange("(p t) n -> p t n", t=PACK)
-        sums = {}
-        for t in range(PACK):
+        halves = [slice(h * HALF, (h + 1) * HALF) for h in range(2)]
+        bank_of = {1: banks[5], 2: banks[6], 3: banks[7]}
+        hw = {0: wide[0], 1: wide[1], 2: wide[2], 3: wide[0]}
+        gate, other = {}, {}
+
+        def rows(t):
             cols = slice(t * M, (t + 1) * M)
             if t == 0:
-                sums[t] = [banks[5][:, :HALF], banks[6][:, :HALF]]
-                for h in range(2):
-                    c = slice(h * HALF, (h + 1) * HALF)
-                    product(sums[t][h], d_codes[:, cols], d_scale[:, cols], z_codes[:, c], z_scales[:, c])
+                for h, c in enumerate(halves):
+                    product(banks[5 + h][:, :HALF], d_codes[:, cols], d_scale[:, cols], z_codes[:, c], z_scales[:, c])
+                    nc.vector.tensor_scalar(hw[t][:, c], banks[5 + h][:, :HALF], 0.0625, None, MULT)
             else:
-                bank = banks[(7, 0, 1)[t - 1]]
-                sums[t] = [bank[:, :HALF], bank[:, HALF:]]
-                product(bank[:], d_codes[:, cols], d_scale[:, cols], z_codes[:], z_scales[:])
+                product(bank_of[t][:], d_codes[:, cols], d_scale[:, cols], z_codes[:], z_scales[:])
+                nc.scalar.activation(hw[t][:, :S], bank_of[t][:], COPY, scale=0.0625)
 
-        halves = [slice(h * HALF, (h + 1) * HALF) for h in range(2)]
-        for t in range(PACK):
-            hw = wide[t]
-            gate = sb(f"gate{t}", [P, S], F32)
-            other = sb(f"other{t}", [P, S], F32)
-            diff = sb(f"diff{t}", [P, S], F32)
-            res = sb(f"res{t}", [P, S], F32)
-            if t == 0:
-                nc.scalar.activation(hw[:, :HALF], sums[t][0], COPY, scale=0.0625)
-                nc.vector.tensor_scalar(hw[:, HALF:S], sums[t][1], 0.0625, None, MULT)
-            else:
-                nc.scalar.activation(hw[:, :S], banks[(7, 0, 1)[t - 1]][:], COPY, scale=0.0625)
-            if t % 2 == 0:
-                nc.vector.tensor_copy(other[:], hw[:].indirect(n3_t[:]))
-            else:
-                nc.vector.tensor_copy(other[:, :HALF], hw[:].indirect(n3_t[:, :16]))
-                nc.scalar.activation(other[:, HALF:], hw[:].indirect(n3_t[:, 16:]), COPY)
+        def look_up_other(t):
+            other[t] = sb(f"other{t}", [P, S], F32)
+            for h, c in enumerate(halves):
+                nc.vector.tensor_copy(other[t][:, c], hw[t][:].indirect(n3_t[:, h * 16 : (h + 1) * 16]))
+
+        def look_up_gate(t):
+            gate[t] = sb(f"gate{t}", [P, S], F32)
             if t < PACK - 1:
-                nc.scalar.activation(gate[:], hw[:].indirect(n4_t[:]), SIGMOID)
+                nc.scalar.activation(gate[t][:], hw[t][:].indirect(n4_t[:]), SIGMOID)
+            else:
+                for h, c in enumerate(halves):
+                    nc.scalar.activation(gate[t][:, c], hw[t][:].indirect(n4_t[:, h * 16 : (h + 1) * 16]), SIGMOID)
+
+        def finish(t):
+            res = sb(f"res{t}", [P, S], F32)
+            diff = sb(f"diff{t}", [P, S], F32)
+            for c in halves:
                 if t == 0:
-                    for h, c in enumerate(halves):
-                        nc.vector.scalar_tensor_tensor(diff[:, c], sums[t][h], 0.0625, other[:, c], MULT, SUB)
+                    nc.vector.tensor_tensor(diff[:, c], hw[t][:, c], other[t][:, c], SUB)
                 else:
-                    nc.vector.scalar_tensor_tensor(diff[:], banks[(7, 0, 1)[t - 1]][:], 0.0625, other[:], MULT, SUB)
-                nc.vector.tensor_tensor(res[:], diff[:], gate[:], MULT)
+                    nc.vector.scalar_tensor_tensor(diff[:, c], bank_of[t][:, c], 0.0625, other[t][:, c], MULT, SUB)
+            if t < PACK - 1:
+                nc.gpsimd.tensor_tensor(res[:], diff[:], gate[t][:], MULT)
                 nc.sync.dma_start(out_rows[:, t, :], res[:])
             else:
-                for h, c in enumerate(halves):
-                    nc.scalar.activation(gate[:, c], hw[:].indirect(n4_t[:, h * 16 : (h + 1) * 16]), SIGMOID)
-                for h, c in enumerate(halves):
-                    nc.vector.scalar_tensor_tensor(diff[:, c], sums[t][h], 0.0625, other[:, c], MULT, SUB)
-                for h, c in enumerate(halves):
-                    nc.vector.tensor_tensor(res[:, c], diff[:, c], gate[:, c], MULT)
+                for c in halves:
+                    nc.vector.tensor_tensor(res[:, c], diff[:, c], gate[t][:, c], MULT)
                     nc.sync.dma_start(out_rows[:, t, c], res[:, c])
+
+        rows(0)
+        look_up_gate(0)
+        look_up_other(0)
+        rows(1)
+        finish(0)
+        look_up_other(1)
+        rows(2)
+        look_up_gate(1)
+        finish(1)
+        look_up_other(2)
+        rows(3)
+        look_up_gate(2)
+        finish(2)
+        look_up_other(3)
+        look_up_gate(3)
+        finish(3)

@@ -55,6 +55,9 @@ def tile_picked_densehaargdif_none_p_kernel(
         nc.vector.memset(ds[:].bitcast(I32), 0)
         nc.vector.memset(d_scale[:].bitcast(I32), 0)
 
+        warm = sb("warm", [P, 2], F32)
+        nc.vector.memset(warm[:, 0:1], 0.0)
+        nc.scalar.activation(warm[:, 1:2], warm[:, 0:1], SIGMOID)
         nc.sync.dma_start(offs_t[:], offs)
         nc.sync.dma_start(w_raw[:], w1.rearrange("(p j) c -> p j c", j=PACK))
         for q in range(4):

from contextlib import ExitStack

import concourse.mybir as mybir

K, T, S, H, W, G = 512, 2048, 512, 512, 256, 2048
FLOPS = 2 * K * H * S + 2 * K * H * S

F32 = mybir.dt.float32
BF16 = mybir.dt.bfloat16
I32 = mybir.dt.int32
U32 = mybir.dt.uint32
U16 = mybir.dt.uint16
U8 = mybir.dt.uint8
FP8X4 = mybir.dt.float8_e4m3fn_x4
ADD = mybir.AluOpType.add
SUB = mybir.AluOpType.subtract
MULT = mybir.AluOpType.mult
COPY = mybir.ActivationFunctionType.Copy
SIGMOID = mybir.ActivationFunctionType.Sigmoid

P = 128
PACK = 4
HALF = S // 2
M = 128


def tile_picked_densehaargdif_none_p_kernel(
    tc, x_words, x_scales, w1, gs, d_words, d_scales, offs, n1, n2, k1, n3, n4, out
):
    nc = tc.nc
    with ExitStack() as ctx:
        lists = ctx.enter_context(tc.tile_pool(name="lists", bufs=1))
        keep = ctx.enter_context(tc.tile_pool(name="keep", bufs=1))
        psum = ctx.enter_context(tc.psum_pool(name="psum", bufs=1))

        def sb(name, shape, dtype, tag=None):
            return keep.tile(shape, dtype, name=name, tag=tag or name, align_bytes=64)

        offs_t = lists.tile([P, S // 16], U16, name="offs_t")
        n1_t = lists.tile([P, W // 16], U16, name="n1_t")
        n2_t = lists.tile([P, W // 16], U16, name="n2_t")
        k1_t = lists.tile([P, H // 16], U16, name="k1_t")
        n3_t = lists.tile([P, S // 16], U16, name="n3_t")
        n4_t = lists.tile([P, S // 16], U16, name="n4_t")

        w_raw = sb("w_raw", [P, PACK, H], F32)
        xw = sb("xw", [P, T], U32)
        xs = sb("xs", [P, T], U8)
        dw = sb("dw", [P, G], U32)
        ds = sb("ds", [P, G], U8)
        gain = sb("gain", [P, PACK], F32)
        d_scale = sb("d_scale", [P, H], U8)

        nc.gpsimd.memset(xs[:].bitcast(I32), 0)
        nc.vector.memset(ds[:].bitcast(I32), 0)
        nc.vector.memset(d_scale[:].bitcast(I32), 0)

        warm = sb("warm", [P, 2], F32)
        nc.vector.memset(warm[:, 0:1], 0.0)
        nc.scalar.activation(warm[:, 1:2], warm[:, 0:1], SIGMOID)
        nc.sync.dma_start(offs_t[:], offs)
        nc.sync.dma_start(w_raw[:], w1.rearrange("(p j) c -> p j c", j=PACK))
        for q in range(4):
            nc.sync.dma_start(
                xs[32 * q : 32 * q + 4, :].bitcast(I32), x_scales[0, 4 * q : 4 * q + 4, :].bitcast(I32)
            )
        nc.sync.dma_start(xw[:].bitcast(I32), x_words[0].rearrange("p n t -> p (n t)").bitcast(I32))
        nc.sync.dma_start(k1_t[:], k1)
        d_rows = d_scales[0].rearrange("(r s) c -> s r c", s=2)
        for s in range(2):
            nc.sync.dma_start(ds[s:P:16, :].bitcast(I32), d_rows[s].bitcast(I32))
        nc.sync.dma_start(gain[:], gs.rearrange("(p t) o -> p (t o)", t=PACK))
        nc.sync.dma_start(n1_t[:], n1)
        nc.sync.dma_start(n2_t[:], n2)
        nc.sync.dma_start(dw[:].bitcast(I32), d_words[0].rearrange("p n t -> p (n t)").bitcast(I32))
        nc.sync.dma_start(n3_t[:], n3)
        nc.sync.dma_start(n4_t[:], n4)

        x_scale = sb("x_scale", [P, S], U8)
        nc.vector.tensor_copy(x_scale[:], xs[:].indirect(offs_t[:]))

        w_view = w_raw[:].rearrange("p j (m a e) -> p e m j a", a=2, e=2)
        w_codes, w_scales, w_bf = {}, {}, {}
        for e in (1, 0):
            w_bf[e] = sb(f"w_bf{e}", [P, 2 * M * PACK], BF16)
            w_codes[e] = sb(f"w_codes{e}", [P, 2 * M], U32)
            w_scales[e] = sb(f"w_scales{e}", [P, 2 * M], U8)
        nc.vector.tensor_copy(w_bf[1][:].rearrange("p (a m j) -> p m j a", a=2, j=PACK), w_view[:, 1])
        nc.scalar.copy(w_bf[0][:].rearrange("p (a m j) -> p m j a", a=2, j=PACK), w_view[:, 0])
        for e in (1, 0):
            nc.vector.quantize_mx(out=w_codes[e][:].bitcast(FP8X4), scales=w_scales[e][:], in_=w_bf[e][:])

        x_codes = sb("x_codes", [P, S], U32)
        for h in range(2):
            nc.vector.tensor_copy(
                x_codes[:, h * HALF : (h + 1) * HALF], xw[:].indirect(offs_t[:, h * 16 : (h + 1) * 16])
            )

        banks = [psum.tile([P, S], F32, name=f"bank{b}") for b in range(8)]

        def product(bank_cols, lhs_codes, lhs_scales, rhs_codes, rhs_scales):
            nc.tensor.matmul_mx(
                out=bank_cols,
                lhsT=lhs_codes.bitcast(FP8X4),
                lhsT_scale=lhs_scales,
                rhs=rhs_codes.bitcast(FP8X4),
                rhs_scale=rhs_scales,
                start=True,
                stop=True,
            )

        y, first, second, wide, dt = {}, {}, {}, {}, {}

        def project(t):
            e, a = t % 2, t // 2
            cols = slice(a * M, (a + 1) * M)
            y[t] = sb(f"y{t}", [P, S], F32)
            if t == 1:
                for h in range(2):
                    c = slice(h * HALF, (h + 1) * HALF)
                    product(banks[h][:, :HALF], w_codes[e][:, cols], w_scales[e][:, cols], x_codes[:, c], x_scale[:, c])
                    nc.scalar.activation(y[t][:, c], banks[h][:, :HALF], COPY, scale=gain[:, t : t + 1])
            else:
                product(banks[1][:], w_codes[e][:, cols], w_scales[e][:, cols], x_codes[:], x_scale[:])
                nc.scalar.activation(y[t][:], banks[1][:], COPY, scale=gain[:, t : t + 1])

        def fetch(t):
            wide[t] = sb(f"wide{t}", [P, 2 * S], F32)
            first[t] = wide[t][:, S : S + W]
            second[t] = wide[t][:, S + W :]
            if t == 1:
                nc.vector.tensor_copy(first[t], y[t][:].indirect(n1_t[:]))
            else:
                nc.scalar.activation(first[t], y[t][:].indirect(n1_t[:]), COPY)
            nc.scalar.activation(second[t], y[t][:].indirect(n2_t[:]), COPY, scale=-1.0)

        def scale(t):
            scaled[t] = sb(f"scaled{t}", [P, 2 * W], F32)
            nc.scalar.activation(scaled[t][:, :W], first[t], COPY, scale=0.75)
            nc.scalar.activation(scaled[t][:, W:], second[t], COPY, scale=-0.75)

        def put_difference(t):
            nc.vector.tensor_tensor(dt[t][:].indirect(n2_t[:]), first[t], second[t], ADD)

        def put_sum(t):
            nc.vector.tensor_tensor(dt[t][:].indirect(n1_t[:]), scaled[t][:, :W], scaled[t][:, W:], ADD)

        scaled = {}
        project(1)
        ds_picked = sb("ds_picked", [P, H], U8)
        nc.vector.tensor_copy(ds_picked[:], ds[:].indirect(k1_t[:]))
        fetch(1)
        dt[1] = sb("dt1", [P, S], F32, tag="ds")
        dt[3] = sb("dt3", [P, S], F32)
        put_difference(1)
        ds_dealt = sb("ds_dealt", [P, H], U8, tag="y1")
        nc.vector.tensor_copy(
            ds_dealt[:].rearrange("p (t m) -> p m t", t=PACK), ds_picked[:].rearrange("p (m t) -> p m t", t=PACK)
        )
        for o in range(2):
            for s in range(2):
                nc.sync.dma_start(
                    d_scale[2 * o + s : P : 32, :].bitcast(I32), ds_dealt[16 * o + s : P : 32, :].bitcast(I32)
                )
        project(3)
        fetch(3)
        put_difference(3)
        scale(1)
        put_sum(1)
        scale(3)
        put_sum(3)
        project(0)
        fetch(0)
        dt[0] = sb("dt01", [P, 2 * S], F32, tag="y0")
        nc.scalar.copy(dt[0][:, S:], dt[1][:])
        put_difference(0)
        project(2)
        fetch(2)
        dt[2] = sb("dt23", [P, 2 * S], F32, tag="y2")
        nc.scalar.copy(dt[2][:, S:], dt[3][:])
        put_difference(2)
        scale(0)
        put_sum(0)
        scale(2)
        put_sum(2)

        pairs = sb("pairs", [P, 2, S, 2], BF16)
        nc.scalar.copy(pairs[:, 0], dt[0][:].rearrange("p (e n) -> p n e", e=2))
        for h in range(2):
            c = slice(h * HALF, (h + 1) * HALF)
            nc.scalar.copy(pairs[:, 1, c, :], dt[2][:].rearrange("p (e n) -> p n e", e=2)[:, c, :])
        pair_words = pairs[:].rearrange("p a n e -> p (a n e)").bitcast(U32).rearrange("p (a n) -> p n a", a=2)
        z_bf = [sb(f"z_bf{h}", [P, HALF * PACK], BF16) for h in range(2)]
        for h in range(2):
            nc.scalar.copy(
                z_bf[h][:].bitcast(U32).rearrange("p (n a) -> p n a", a=2), pair_words[:, h * HALF : (h + 1) * HALF, :]
            )

        d_picked = sb("d_picked", [P, H], U32, tag="scaled2")
        d_codes = sb("d_codes", [P, H], U32)
        nc.vector.tensor_copy(d_picked[:], dw[:].indirect(k1_t[:]))
        z_codes = sb("z_codes", [P, S], U32)
        z_scales = sb("z_scales", [P, S], U8)
        for h in range(2):
            c = slice(h * HALF, (h + 1) * HALF)
            nc.vector.quantize_mx(
                out=z_codes[:, c].bitcast(FP8X4),
                scales=z_scales[:, c],
                in_=z_bf[h][:],
            )
            if h == 0:
                nc.vector.tensor_copy(
                    d_codes[:].rearrange("p (t m) -> p m t", t=PACK),
                    d_picked[:].rearrange("p (m t) -> p m t", t=PACK),
                )

        out_rows = out.rearrange("(p t) n -> p t n", t=PACK)
        halves = [slice(h * HALF, (h + 1) * HALF) for h in range(2)]
        bank_of = {1: banks[5], 2: banks[6], 3: banks[7]}
        hw = {0: wide[0], 1: wide[1], 2: wide[2], 3: wide[0]}
        gate, other = {}, {}

        def rows(t):
            cols = slice(t * M, (t + 1) * M)
            if t == 0:
                for h, c in enumerate(halves):
                    product(banks[5 + h][:, :HALF], d_codes[:, cols], d_scale[:, cols], z_codes[:, c], z_scales[:, c])
                    nc.vector.tensor_scalar(hw[t][:, c], banks[5 + h][:, :HALF], 0.0625, None, MULT)
            else:
                product(bank_of[t][:], d_codes[:, cols], d_scale[:, cols], z_codes[:], z_scales[:])
                nc.scalar.activation(hw[t][:, :S], bank_of[t][:], COPY, scale=0.0625)

        def look_up_other(t):
            other[t] = sb(f"other{t}", [P, S], F32)
            for h, c in enumerate(halves):
                nc.vector.tensor_copy(other[t][:, c], hw[t][:].indirect(n3_t[:, h * 16 : (h + 1) * 16]))

        def look_up_gate(t):
            gate[t] = sb(f"gate{t}", [P, S], F32)
            if t < PACK - 1:
                nc.scalar.activation(gate[t][:], hw[t][:].indirect(n4_t[:]), SIGMOID)
            else:
                for h, c in enumerate(halves):
                    nc.scalar.activation(gate[t][:, c], hw[t][:].indirect(n4_t[:, h * 16 : (h + 1) * 16]), SIGMOID)

        def finish(t):
            res = sb(f"res{t}", [P, S], F32)
            diff = sb(f"diff{t}", [P, S], F32)
            for c in halves:
                if t == 0:
                    nc.vector.tensor_tensor(diff[:, c], hw[t][:, c], other[t][:, c], SUB)
                else:
                    nc.vector.scalar_tensor_tensor(diff[:, c], bank_of[t][:, c], 0.0625, other[t][:, c], MULT, SUB)
            if t < PACK - 1:
                nc.gpsimd.tensor_tensor(res[:], diff[:], gate[t][:], MULT)
                nc.sync.dma_start(out_rows[:, t, :], res[:])
            else:
                for c in halves:
                    nc.vector.tensor_tensor(res[:, c], diff[:, c], gate[t][:, c], MULT)
                    nc.sync.dma_start(out_rows[:, t, c], res[:, c])

        rows(0)
        look_up_gate(0)
        look_up_other(0)
        rows(1)
        finish(0)
        look_up_other(1)
        rows(2)
        look_up_gate(1)
        finish(1)
        look_up_other(2)
        rows(3)
        look_up_gate(2)
        finish(2)
        look_up_other(3)
        look_up_gate(3)
        finish(3)
